import numpy as np
import ml_dtypes


def mxq(x, axis, fmt="e4m3"):
    dtype, down = {"e4m3": (ml_dtypes.float8_e4m3fn, 7), "e5m2": (ml_dtypes.float8_e5m2, 14)}[fmt]
    v = np.moveaxis(np.asarray(x, np.float32).astype(ml_dtypes.bfloat16).astype(np.float64), axis, -1)
    blocks = v.reshape(v.shape[:-1] + (-1, 32))
    amax = np.abs(blocks).max(-1, keepdims=True)
    byte = np.maximum(np.where(amax > 0, np.frexp(amax)[1] - 1 + 127, 0) - down, 1)
    scale = np.exp2(byte - 127.0)
    codes = (blocks / scale).astype(np.float32).astype(dtype).astype(np.float64)
    return np.moveaxis((codes * scale).reshape(v.shape), -1, axis)


WIDE = False


def mx_kscale(k):
    if not WIDE:
        return np.ones(k)
    levels = np.array([10, -10, 5, -5, 0])
    if k % 512:
        return np.exp2(np.random.permutation(np.resize(levels, k // 32))).repeat(32)
    a = np.empty((k // 512, 16))
    for p in range(k // 512):
        a[p, :8] = np.random.permutation(np.resize(levels, 8))
        for g in range(8):
            far = levels[np.abs(levels - a[p, g]) >= 10]
            a[p, g + 8] = far[np.random.randint(len(far))]
    return np.exp2(a.ravel()).repeat(32)


BF16 = ml_dtypes.bfloat16


def bf(x):
    return np.asarray(x, np.float32).astype(BF16)


def f64(x):
    return np.asarray(x).astype(np.float64)


E2M1 = np.array([0.0, 0.5, 1.0, 1.5, 2.0, 3.0, 4.0, 6.0, -0.0, -0.5, -1.0, -1.5, -2.0, -3.0, -4.0, -6.0])


def pack_weight(w, fmt):
    k, n = w.shape
    w = f64(bf(w)).reshape(k // 32, 32, n)
    amax = np.abs(w).max(1)
    if fmt == "e4m3":
        byte = np.frexp(amax)[1] - 1 + 127 - 7
    else:
        mant, ex = np.frexp(amax / 6.0)
        byte = np.where(mant > 0.5, ex, ex - 1) + 127
    byte = np.clip(np.where(amax > 0, byte, 1), 1, 254)
    scaled = (w * np.exp2(127.0 - byte)[:, None, :]).reshape(k, n).astype(np.float32)
    by_word = np.ascontiguousarray(scaled.reshape(k // 512, 128, 4, n).transpose(0, 1, 3, 2))
    if fmt == "e4m3":
        words = by_word.astype(ml_dtypes.float8_e4m3fn).view(np.uint8)
    else:
        c = by_word.astype(ml_dtypes.float4_e2m1fn).view(np.uint8) & 0xF
        words = c[..., 0::2] | (c[..., 1::2] << 4)
    return np.ascontiguousarray(words), np.ascontiguousarray(byte.astype(np.uint8).reshape(k // 512, 16, n))


def unpack_weight(words, scales, fmt):
    g, p, n, _ = words.shape
    if fmt == "e4m3":
        vals = np.ascontiguousarray(words).view(ml_dtypes.float8_e4m3fn).astype(np.float64)
    else:
        nib = np.empty((g, p, n, 4), np.uint8)
        nib[..., 0::2] = words & 0xF
        nib[..., 1::2] = words >> 4
        vals = E2M1[nib]
    vals = vals * np.repeat(np.exp2(scales.astype(np.float64) - 127.0), 8, axis=1)[..., None]
    return vals.transpose(0, 1, 3, 2).reshape(g * 512, n)
def pack4(w):
    words, scales = pack_weight(w, "e2m1")
    return words.reshape(words.shape[0], 128, -1), scales


def unpack4(words, scales):
    return unpack_weight(words.reshape(words.shape[0], 128, -1, 2), scales, "e2m1")


def planes(Y):
    n, m = Y.shape
    b = f64(bf(Y)).reshape(n // 32, 32, m)
    amax = np.abs(b).max(1)
    byte = np.clip(np.where(amax > 0, np.frexp(amax)[1] - 1 + 127 - 7, 1), 1, 254)
    codes = (b * np.exp2(127.0 - byte)[:, None, :]).reshape(n, m).astype(np.float32).astype(ml_dtypes.float8_e4m3fn).view(np.uint8)
    words = codes.reshape(n // 512, 128, 4, m).transpose(0, 1, 3, 2)
    return np.ascontiguousarray(words), np.ascontiguousarray(byte.astype(np.uint8).reshape(n // 512, 16, m))


B, D, E, Q = 1024, 1024, 1024, 1024


def huber_influence(r):
    return np.maximum(-1.0, np.minimum(1.0, r))


def setup_inputs():
    s = mx_kscale(D)
    u = mx_kscale(B)
    x = bf(np.random.standard_normal((B, D)) * s)
    m_words, m_scales = pack4(np.random.standard_normal((D, E)) / np.sqrt(D) / s[:, None])
    return {"x": x,
            "m_words": m_words,
            "m_scales": m_scales,
            "b": bf(0.5 * np.random.standard_normal(E)),
            "y": bf(np.random.standard_normal((B, E))),
            "c": bf((1.0 + 0.1 * np.random.standard_normal(B)) * u),
            "z": bf(np.random.standard_normal((B, Q)) / u[:, None])}


def core(x, m_words, m_scales, b, y, c, z):
    n = x.shape[0]
    r = (mxq(f64(x), 1, "e4m3") @ unpack4(m_words, m_scales)) + f64(b) - f64(y)
    psi = huber_influence(r)
    t = f64(c)[:, None] * psi
    return (mxq(f64(z), 0, "e4m3").T @ mxq(t, 0, "e4m3")) / np.sqrt(n)


def reference(x, m_words, m_scales, b, y, c, z):
    R_out = core(x, m_words, m_scales, b, y, c, z)
    words, scales = planes(R_out)
    return R_out, words, scales

@@ -1,0 +1,336 @@
+from contextlib import ExitStack
+
+import concourse.mybir as mybir
+from concourse.masks import make_identity
+
+B, D, E, Q = 1024, 1024, 1024, 1024
+FLOPS = 2 * B * D * E + 2 * B * Q * E
+
+F32 = mybir.dt.float32
+BF16 = mybir.dt.bfloat16
+I32 = mybir.dt.int32
+U32 = mybir.dt.uint32
+U8 = mybir.dt.uint8
+FP8X4 = mybir.dt.float8_e4m3fn_x4
+FP4X4 = mybir.dt.float4_e2m1fn_x4
+ALU = mybir.AluOpType
+ACT = mybir.ActivationFunctionType
+
+P = 128
+PACK = 4
+GROUP = P * PACK
+HALF = 512
+OUT_SCALE = 1.0 / 32.0
+
+
+def tile_iv4rechubermomentmatrix_x2_kernel(tc, x, m_words, m_scales, b, y, c, z, out_0, out_1, out_2):
+    nc = tc.nc
+    V, S, G = nc.vector, nc.scalar, nc.gpsimd
+
+    with ExitStack() as ctx:
+        keep = ctx.enter_context(tc.tile_pool(name="keep", bufs=1))
+        stage = ctx.enter_context(tc.tile_pool(name="stage", bufs=3))
+        psum = ctx.enter_context(tc.psum_pool(name="psum", bufs=1))
+        ctx.enter_context(tc.manual_schedule(engines={mybir.EngineType.SP}))
+
+        def kept(name, shape, dtype):
+            return keep.tile(shape, dtype, name=name, align_bytes=64)
+
+        def copy_on(engine, out, in_):
+            if engine is S:
+                S.copy(out=out, in_=in_)
+            elif engine is G:
+                G.tensor_scalar(out=out, in0=in_, scalar1=1.0, scalar2=0.0, op0=ALU.mult, op1=ALU.add)
+            else:
+                V.tensor_copy(out=out, in_=in_)
+
+        ident = kept("ident", [P, P], F32)
+        c_row = kept("c_row", [P, B], BF16)
+        b_row = kept("b_row", [P, E], BF16)
+        c_col = kept("c_col", [P, 2 * PACK], BF16)
+        c_neg = kept("c_neg", [P, 2 * PACK], F32)
+        c_abs = kept("c_abs", [P, 2 * PACK], F32)
+        c_abs_neg = kept("c_abs_neg", [P, 2 * PACK], F32)
+        m_plane = kept("m_plane", [P, 2, E], U8)
+        out_plane = kept("out_plane", [P, E], U8)
+
+        x_rows, y_rows, z_rows, m_codes, diags = {}, {}, {}, {}, {}
+        x_woven, x_codes, x_planes = {}, {}, {}
+        offsets, scaled, t_rows, t_woven, t_codes, t_planes = {}, {}, {}, {}, {}, {}
+        z_woven, z_codes, z_planes = {}, {}, {}
+        results, out_woven, out_codes = {}, {}, {}
+
+        V.memset(c_row[:].bitcast(I32), 0)
+        V.memset(b_row[:].bitcast(I32), 0)
+        V.memset(m_plane[:].rearrange("p g e -> p (g e)").bitcast(I32), 0)
+        make_identity(nc, ident[:])
+
+        def sample_rows(src, g):
+            return src[GROUP * g : GROUP * (g + 1), :].rearrange("(p j) w -> p j w", j=PACK)
+
+        def load_rows():
+            nc.sync.dma_start(out=c_row[0:1, :], in_=c.rearrange("(o n) -> o n", o=1))
+            nc.sync.dma_start(out=b_row[0:1, :], in_=b.rearrange("(o n) -> o n", o=1))
+            nc.sync.dma_start(
+                out=c_col[:].rearrange("p (g j) -> p g j", g=2),
+                in_=c.rearrange("(g p j) -> p g j", g=2, j=PACK),
+            )
+
+        def load_slots(src, name, table, g, j0, j1):
+            rows = kept("%s%d%d" % (name, g, j0), [P, j1 - j0, src.shape[1]], BF16)
+            nc.sync.dma_start(out=rows[:], in_=sample_rows(src, g)[:, j0:j1, :])
+            for j in range(j0, j1):
+                table[g, j] = rows[:, j - j0, :]
+
+        def load_x(g, j0, j1):
+            load_slots(x, "x", x_rows, g, j0, j1)
+
+        def load_y(g, j0, j1):
+            load_slots(y, "y", y_rows, g, j0, j1)
+
+        def load_z(g, q):
+            z_rows[g, q] = kept("z%d%d" % (g, q), [P, PACK, GROUP], BF16)
+            nc.sync.dma_start(out=z_rows[g, q][:], in_=sample_rows(z, g)[:, :, GROUP * q : GROUP * (q + 1)])
+
+        def load_m(h):
+            m_codes[h] = kept("m%d" % h, [P, 2, 2 * HALF], U8)
+            src = m_words.rearrange("k p w -> p k w")[:, :, 2 * HALF * h : 2 * HALF * (h + 1)]
+            nc.sync.dma_start(out=m_codes[h][:].bitcast(I32), in_=src.bitcast(I32))
+
+        def load_m_scales():
+            for quad in range(4):
+                src = m_scales[:, 4 * quad : 4 * quad + 4, :].rearrange("k r e -> r k e")
+                nc.sync.dma_start(out=m_plane[32 * quad : 32 * quad + 4, :, :].bitcast(I32), in_=src.bitcast(I32))
+
+        def weights():
+            S.activation(out=c_abs[:], in_=c_col[:], func=ACT.Abs)
+            V.tensor_scalar(out=c_neg[:], in0=c_col[:], scalar1=-1.0, scalar2=None, op0=ALU.mult)
+            V.tensor_scalar(out=c_abs_neg[:], in0=c_abs[:], scalar1=-1.0, scalar2=None, op0=ALU.mult)
+
+        def column(tile, g, j):
+            return tile[:, PACK * g + j : PACK * g + j + 1]
+
+        def diag(g, j):
+            diags[g, j] = kept("diag%d%d" % (g, j), [P, P], BF16)
+            V.tensor_scalar(out=diags[g, j][:], in0=ident[:], scalar1=column(c_neg, g, j), scalar2=None, op0=ALU.mult)
+
+        def make_offset(g, h, j, engine):
+            cols = slice(HALF * h, HALF * (h + 1))
+            bank = psum.tile([P, HALF], F32, name="offset_bank", bufs=2)
+            offsets[g, h, j] = kept("offset%d%d%d" % (g, h, j), [P, HALF], F32)
+            c_slot = c_row[:, GROUP * g + j : GROUP * (g + 1) : PACK]
+            if engine is S:
+                nc.tensor.matmul(bank[:], lhsT=c_slot, rhs=b_row[:, cols], start=True, stop=False)
+                nc.tensor.matmul(bank[:], lhsT=diags[g, j][:], rhs=y_rows[g, j][:, cols], start=False, stop=True)
+                S.copy(out=offsets[g, h, j][:], in_=bank[:])
+            else:
+                nc.tensor.matmul(bank[:], lhsT=c_slot, rhs=b_row[:, cols], start=True, stop=True)
+                V.scalar_tensor_tensor(
+                    out=offsets[g, h, j][:], in0=y_rows[g, j][:, cols], scalar=column(c_neg, g, j),
+                    in1=bank[:], op0=ALU.mult, op1=ALU.add,
+                )
+
+        def turn_x(g, j):
+            bank = psum.tile([P, HALF], F32, name="shared_bank", bufs=3)
+            pairs = x_rows[g, j].bitcast(F32)
+            for k in range(2):
+                for u in range(2):
+                    at = P * (2 * k + u)
+                    nc.tensor.transpose(bank[:, at : at + P], pairs[:, 256 * k + u : 256 * (k + 1) : 2], ident[:])
+            x_woven[g, j] = stage.tile([P, D], BF16, name="x_woven", bufs=4, align_bytes=64)
+            S.copy(
+                out=x_woven[g, j][:].bitcast(F32).rearrange("p (k n u) -> p k n u", k=2, u=2),
+                in_=bank[:].rearrange("p (k u n) -> p k n u", k=2, u=2),
+            )
+
+        def quantize(codes, plane, woven):
+            V.quantize_mx(out=codes.bitcast(FP8X4), scales=plane, in_=woven)
+
+        def quant_x(g, j):
+            x_codes[g, j] = kept("x_codes%d%d" % (g, j), [P, 2 * P], U32)
+            x_planes[g, j] = kept("x_plane%d%d" % (g, j), [P, 2 * P], U8)
+            quantize(x_codes[g, j][:], x_planes[g, j][:], x_woven[g, j][:])
+
+        def residual(g, h, j):
+            bank = psum.tile([P, HALF], F32, name="residual_bank", bufs=3)
+            for k in range(2):
+                nc.tensor.matmul_mx(
+                    out=bank[:],
+                    lhsT=x_codes[g, j][:, P * k : P * (k + 1)].bitcast(FP8X4),
+                    lhsT_scale=x_planes[g, j][:, P * k : P * (k + 1)],
+                    rhs=m_codes[h][:, k, :].bitcast(FP4X4),
+                    rhs_scale=m_plane[:, k, HALF * h : HALF * (h + 1)],
+                    start=(k == 0),
+                    stop=(k == 1),
+                )
+            scaled[g, h, j] = stage.tile([P, HALF], F32, name="scaled", bufs=4)
+            V.scalar_tensor_tensor(
+                out=scaled[g, h, j][:], in0=bank[:], scalar=column(c_col, g, j),
+                in1=offsets[g, h, j][:], op0=ALU.mult, op1=ALU.add,
+            )
+
+        def clip(g, h, j, engine=V):
+            if j == 0:
+                t_rows[g, h] = stage.tile([P, PACK, HALF], BF16, name="t_rows", bufs=3)
+            engine.tensor_scalar(
+                out=t_rows[g, h][:, j, :], in0=scaled[g, h, j][:],
+                scalar1=column(c_abs, g, j), scalar2=column(c_abs_neg, g, j), op0=ALU.min, op1=ALU.max,
+            )
+
+        def weave(engine, woven, rows, c0, c1):
+            copy_on(
+                engine,
+                woven[:].rearrange("p (w i j) -> p w j i", i=4, j=PACK)[:, c0 // 4 : c1 // 4],
+                rows[:].rearrange("p j (w i) -> p w j i", i=4)[:, c0 // 4 : c1 // 4],
+            )
+
+        def weave_t(g, h, engine, c0=0, c1=HALF):
+            if c0 == 0:
+                t_woven[g, h] = stage.tile([P, PACK * HALF], BF16, name="t_woven", bufs=2, align_bytes=64)
+            weave(engine, t_woven[g, h], t_rows[g, h], c0, c1)
+
+        def quant_t(g, h):
+            t_codes[g, h] = kept("t_codes%d%d" % (g, h), [P, HALF], U32)
+            t_planes[g, h] = kept("t_plane%d%d" % (g, h), [P, HALF], U8)
+            quantize(t_codes[g, h][:], t_planes[g, h][:], t_woven[g, h][:])
+
+        def weave_z(g, q, engine, c0=0, c1=P):
+            if c0 == 0:
+                z_woven[g, q] = stage.tile([P, PACK * HALF], BF16, name="z_woven", bufs=3, align_bytes=64)
+            copy_on(
+                engine,
+                z_woven[g, q][:].rearrange("p (t m j) -> p m j t", t=PACK, j=PACK)[:, c0:c1],
+                z_rows[g, q][:].rearrange("p j (m t) -> p m j t", t=PACK)[:, c0:c1],
+            )
+
+        def quant_z(g, q):
+            z_codes[g, q] = kept("z_codes%d%d" % (g, q), [P, GROUP], U32)
+            z_planes[g, q] = kept("z_plane%d%d" % (g, q), [P, GROUP], U8)
+            quantize(z_codes[g, q][:], z_planes[g, q][:], z_woven[g, q][:])
+
+        def moment(h, q, t, engine=S):
+            bank = psum.tile([P, HALF], F32, name="shared_bank", bufs=3)
+            for g in range(2):
+                nc.tensor.matmul_mx(
+                    out=bank[:],
+                    lhsT=z_codes[g, q][:, P * t : P * (t + 1)].bitcast(FP8X4),
+                    lhsT_scale=z_planes[g, q][:, P * t : P * (t + 1)],
+                    rhs=t_codes[g, h][:].bitcast(FP8X4),
+                    rhs_scale=t_planes[g, h][:],
+                    start=(g == 0),
+                    stop=(g == 1),
+                )
+            if t == 0:
+                results[h, q] = kept("result%d%d" % (h, q), [P, PACK, HALF], F32)
+            if engine is S:
+                S.activation(out=results[h, q][:, t, :], in_=bank[:], func=ACT.Copy, scale=OUT_SCALE)
+            else:
+                V.tensor_scalar(out=results[h, q][:, t, :], in0=bank[:], scalar1=OUT_SCALE, scalar2=None, op0=ALU.mult)
+
+        def store_out(h, q, t0, t1):
+            dst = sample_rows(out_0, q)[:, t0:t1, HALF * h : HALF * (h + 1)]
+            nc.sync.dma_start(out=dst, in_=results[h, q][:, t0:t1, :])
+
+        def weave_out(h, q, engine, c0=0, c1=HALF):
+            if c0 == 0:
+                out_woven[h, q] = stage.tile([P, PACK * HALF], BF16, name="out_woven", bufs=3, align_bytes=64)
+            weave(engine, out_woven[h, q], results[h, q], c0, c1)
+
+        def quant_out(h, q, c0=0, c1=HALF):
+            if c0 == 0:
+                out_codes[h, q] = kept("out_codes%d%d" % (h, q), [P, HALF], U32)
+            quantize(
+                out_codes[h, q][:, c0:c1],
+                out_plane[4 * q : P, HALF * h + c0 : HALF * h + c1],
+                out_woven[h, q][:, PACK * c0 : PACK * c1],
+            )
+
+        def store_words(h, q, c0=0, c1=HALF):
+            dst = out_1[q].rearrange("p e t -> p (e t)")[:, PACK * (HALF * h + c0) : PACK * (HALF * h + c1)]
+            nc.sync.dma_start(out=dst.bitcast(I32), in_=out_codes[h, q][:, c0:c1].bitcast(I32))
+
+        def store_scales():
+            for quad in range(4):
+                nc.sync.dma_start(
+                    out=out_2[:, 4 * quad : 4 * quad + 4, :].bitcast(I32),
+                    in_=out_plane[32 * quad : 32 * quad + 8, :].bitcast(I32),
+                )
+
+        load_rows()
+        load_x(0, 0, 1)
+        load_x(0, 1, 2)
+        load_x(0, 2, 4)
+        load_m(0)
+        load_y(0, 0, 2)
+        load_m_scales()
+        load_y(0, 2, 4)
+        load_m(1)
+        load_z(0, 0)
+        load_x(1, 0, 2)
+        load_x(1, 2, 4)
+        load_y(1, 0, 2)
+        load_y(1, 2, 4)
+        load_z(1, 0)
+        load_z(0, 1)
+        load_z(1, 1)
+        weights()
+        for g in range(2):
+            for j in range(4):
+                if j >= min([2,2,2,2][2 * g], [2,2,2,2][2 * g + 1]):
+                    diag(g, j)
+
+        def x_group(g):
+            for j in range(4):
+                turn_x(g, j)
+                quant_x(g, j)
+
+        def block(g, h, first_on_scalar):
+            for j in range(4):
+                make_offset(g, h, j, V if j < first_on_scalar else S)
+                residual(g, h, j)
+                clip(g, h, j, V)
+
+        def finish_t(g, h, first, second):
+            weave_t(g, h, first, 0, 256)
+            weave_t(g, h, second, 256, 512)
+            quant_t(g, h)
+
+        def finish_z(g, q, first, second):
+            weave_z(g, q, first, 0, 64)
+            weave_z(g, q, second, 64, 128)
+            quant_z(g, q)
+
+        def products(h, q):
+            for t in range(4):
+                moment(h, q, t)
+                if t % 2 == 1:
+                    store_out(h, q, t - 1, t + 1)
+
+        def planes(h, q):
+            weave_out(h, q, V)
+            quant_out(h, q)
+            store_words(h, q)
+
+        x_group(0)
+        block(0, 0, 2)
+        x_group(1)
+        block(0, 1, 2)
+        block(1, 0, 2)
+        finish_t(0, 0, S, S)
+        finish_z(0, 0, S, S)
+        finish_z(1, 0, S, S)
+        finish_t(1, 0, V, S)
+        products(0, 0)
+        block(1, 1, 2)
+        finish_z(0, 1, S, S)
+        finish_z(1, 1, S, V)
+        finish_t(0, 1, S, S)
+        finish_t(1, 1, V, V)
+        products(0, 1)
+        planes(0, 0)
+        products(1, 0)
+        planes(0, 1)
+        products(1, 1)
+        planes(1, 0)
+        planes(1, 1)
+        store_scales()

@@ -31,7 +31,7 @@ def tile_iv4rechubermomentmatrix_x2_kernel(tc, x, m_words, m_scales, b, y, c, z,
         keep = ctx.enter_context(tc.tile_pool(name="keep", bufs=1))
         stage = ctx.enter_context(tc.tile_pool(name="stage", bufs=3))
         psum = ctx.enter_context(tc.psum_pool(name="psum", bufs=1))
-        ctx.enter_context(tc.manual_schedule(engines={mybir.EngineType.SP}))
+        ctx.enter_context(tc.manual_schedule(engines={mybir.EngineType.SP, mybir.EngineType.Pool}))
 
         def kept(name, shape, dtype):
             return keep.tile(shape, dtype, name=name, align_bytes=64)
@@ -62,7 +62,7 @@ def tile_iv4rechubermomentmatrix_x2_kernel(tc, x, m_words, m_scales, b, y, c, z,
 
         V.memset(c_row[:].bitcast(I32), 0)
         V.memset(b_row[:].bitcast(I32), 0)
-        V.memset(m_plane[:].rearrange("p g e -> p (g e)").bitcast(I32), 0)
+        G.memset(m_plane[:].rearrange("p g e -> p (g e)").bitcast(I32), 0)
         make_identity(nc, ident[:])
 
         def sample_rows(src, g):
@@ -71,7 +71,9 @@ def tile_iv4rechubermomentmatrix_x2_kernel(tc, x, m_words, m_scales, b, y, c, z,
         def load_rows():
             nc.sync.dma_start(out=c_row[0:1, :], in_=c.rearrange("(o n) -> o n", o=1))
             nc.sync.dma_start(out=b_row[0:1, :], in_=b.rearrange("(o n) -> o n", o=1))
-            nc.sync.dma_start(
+
+        def load_c_col(engine):
+            engine.dma_start(
                 out=c_col[:].rearrange("p (g j) -> p g j", g=2),
                 in_=c.rearrange("(g p j) -> p g j", g=2, j=PACK),
             )
@@ -97,10 +99,10 @@ def tile_iv4rechubermomentmatrix_x2_kernel(tc, x, m_words, m_scales, b, y, c, z,
             src = m_words.rearrange("k p w -> p k w")[:, :, 2 * HALF * h : 2 * HALF * (h + 1)]
             nc.sync.dma_start(out=m_codes[h][:].bitcast(I32), in_=src.bitcast(I32))
 
-        def load_m_scales():
+        def load_m_scales(engine):
             for quad in range(4):
                 src = m_scales[:, 4 * quad : 4 * quad + 4, :].rearrange("k r e -> r k e")
-                nc.sync.dma_start(out=m_plane[32 * quad : 32 * quad + 4, :, :].bitcast(I32), in_=src.bitcast(I32))
+                engine.dma_start(out=m_plane[32 * quad : 32 * quad + 4, :, :].bitcast(I32), in_=src.bitcast(I32))
 
         def weights():
             S.activation(out=c_abs[:], in_=c_col[:], func=ACT.Abs)
@@ -116,7 +118,7 @@ def tile_iv4rechubermomentmatrix_x2_kernel(tc, x, m_words, m_scales, b, y, c, z,
 
         def make_offset(g, h, j, engine):
             cols = slice(HALF * h, HALF * (h + 1))
-            bank = psum.tile([P, HALF], F32, name="offset_bank", bufs=2)
+            bank = psum.tile([P, HALF], F32, name="offset_bank", bufs=3)
             offsets[g, h, j] = kept("offset%d%d%d" % (g, h, j), [P, HALF], F32)
             c_slot = c_row[:, GROUP * g + j : GROUP * (g + 1) : PACK]
             if engine is S:
@@ -131,7 +133,7 @@ def tile_iv4rechubermomentmatrix_x2_kernel(tc, x, m_words, m_scales, b, y, c, z,
                 )
 
         def turn_x(g, j):
-            bank = psum.tile([P, HALF], F32, name="shared_bank", bufs=3)
+            bank = psum.tile([P, HALF], F32, name="turn_bank", bufs=2)
             pairs = x_rows[g, j].bitcast(F32)
             for k in range(2):
                 for u in range(2):
@@ -199,8 +201,8 @@ def tile_iv4rechubermomentmatrix_x2_kernel(tc, x, m_words, m_scales, b, y, c, z,
                 z_woven[g, q] = stage.tile([P, PACK * HALF], BF16, name="z_woven", bufs=3, align_bytes=64)
             copy_on(
                 engine,
-                z_woven[g, q][:].rearrange("p (t m j) -> p m j t", t=PACK, j=PACK)[:, c0:c1],
-                z_rows[g, q][:].rearrange("p j (m t) -> p m j t", t=PACK)[:, c0:c1],
+                z_woven[g, q][:].rearrange("p (t m i j) -> p m t i j", t=PACK, i=2, j=PACK)[:, c0 // 2 : c1 // 2],
+                z_rows[g, q][:].rearrange("p j (m i t) -> p m t i j", i=2, t=PACK)[:, c0 // 2 : c1 // 2],
             )
 
         def quant_z(g, q):
@@ -209,7 +211,8 @@ def tile_iv4rechubermomentmatrix_x2_kernel(tc, x, m_words, m_scales, b, y, c, z,
             quantize(z_codes[g, q][:], z_planes[g, q][:], z_woven[g, q][:])
 
         def moment(h, q, t, engine=S):
-            bank = psum.tile([P, HALF], F32, name="shared_bank", bufs=3)
+            tag, depth = (("turn_bank", 2), ("offset_bank", 3), ("residual_bank", 3) if h else ("turn_bank", 2), ("offset_bank", 3))[t]
+            bank = psum.tile([P, HALF], F32, name=tag, bufs=depth)
             for g in range(2):
                 nc.tensor.matmul_mx(
                     out=bank[:],
@@ -251,18 +254,20 @@ def tile_iv4rechubermomentmatrix_x2_kernel(tc, x, m_words, m_scales, b, y, c, z,
 
         def store_scales():
             for quad in range(4):
-                nc.sync.dma_start(
+                nc.scalar.dma_start(
                     out=out_2[:, 4 * quad : 4 * quad + 4, :].bitcast(I32),
                     in_=out_plane[32 * quad : 32 * quad + 8, :].bitcast(I32),
                 )
 
+        load_c_col(G)
+        load_m_scales(G)
         load_rows()
+        load_y(0, 0, 1)
         load_x(0, 0, 1)
+        load_y(0, 1, 2)
         load_x(0, 1, 2)
-        load_x(0, 2, 4)
         load_m(0)
-        load_y(0, 0, 2)
-        load_m_scales()
+        load_x(0, 2, 4)
         load_y(0, 2, 4)
         load_m(1)
         load_z(0, 0)
@@ -276,7 +281,7 @@ def tile_iv4rechubermomentmatrix_x2_kernel(tc, x, m_words, m_scales, b, y, c, z,
         weights()
         for g in range(2):
             for j in range(4):
-                if j >= min([2,2,2,2][2 * g], [2,2,2,2][2 * g + 1]):
+                if j >= min([4,2,2,2][2 * g], [4,2,2,2][2 * g + 1]):
                     diag(g, j)
 
         def x_group(g):
@@ -312,25 +317,28 @@ def tile_iv4rechubermomentmatrix_x2_kernel(tc, x, m_words, m_scales, b, y, c, z,
             store_words(h, q)
 
         x_group(0)
-        block(0, 0, 2)
+        block(0, 0, 4)
         x_group(1)
         block(0, 1, 2)
         block(1, 0, 2)
-        finish_t(0, 0, S, S)
+        finish_t(0, 0, S, V)
         finish_z(0, 0, S, S)
         finish_z(1, 0, S, S)
         finish_t(1, 0, V, S)
         products(0, 0)
         block(1, 1, 2)
         finish_z(0, 1, S, S)
-        finish_z(1, 1, S, V)
-        finish_t(0, 1, S, S)
-        finish_t(1, 1, V, V)
+        finish_z(1, 1, S, S)
+        finish_t(0, 1, S, V)
+        finish_t(1, 1, V, S)
         products(0, 1)
         planes(0, 0)
         products(1, 0)
         planes(0, 1)
         products(1, 1)
         planes(1, 0)
-        planes(1, 1)
+        weave_out(1, 1, V, 0, 320)
+        weave_out(1, 1, S, 320, 512)
+        quant_out(1, 1)
+        store_words(1, 1)
         store_scales()

@@ -31,7 +31,7 @@ def tile_iv4rechubermomentmatrix_x2_kernel(tc, x, m_words, m_scales, b, y, c, z,
         keep = ctx.enter_context(tc.tile_pool(name="keep", bufs=1))
         stage = ctx.enter_context(tc.tile_pool(name="stage", bufs=3))
         psum = ctx.enter_context(tc.psum_pool(name="psum", bufs=1))
-        ctx.enter_context(tc.manual_schedule(engines={mybir.EngineType.SP, mybir.EngineType.Pool}))
+        ctx.enter_context(tc.manual_schedule())
 
         def kept(name, shape, dtype):
             return keep.tile(shape, dtype, name=name, align_bytes=64)
@@ -62,7 +62,7 @@ def tile_iv4rechubermomentmatrix_x2_kernel(tc, x, m_words, m_scales, b, y, c, z,
 
         V.memset(c_row[:].bitcast(I32), 0)
         V.memset(b_row[:].bitcast(I32), 0)
-        G.memset(m_plane[:].rearrange("p g e -> p (g e)").bitcast(I32), 0)
+        V.memset(m_plane[:].rearrange("p g e -> p (g e)").bitcast(I32), 0)
         make_identity(nc, ident[:])
 
         def sample_rows(src, g):
@@ -91,8 +91,15 @@ def tile_iv4rechubermomentmatrix_x2_kernel(tc, x, m_words, m_scales, b, y, c, z,
             load_slots(y, "y", y_rows, g, j0, j1)
 
         def load_z(g, q):
-            z_rows[g, q] = kept("z%d%d" % (g, q), [P, PACK, GROUP], BF16)
-            nc.sync.dma_start(out=z_rows[g, q][:], in_=sample_rows(z, g)[:, :, GROUP * q : GROUP * (q + 1)])
+            rows = kept("z%d%d" % (g, q), [P, PACK, GROUP], BF16)
+            z_rows[g, q] = rows[:]
+            nc.sync.dma_start(out=rows[:], in_=sample_rows(z, g)[:, :, GROUP * q : GROUP * (q + 1)])
+
+        def load_z_group(g):
+            rows = kept("z%d" % g, [P, PACK, Q], BF16)
+            nc.sync.dma_start(out=rows[:], in_=sample_rows(z, g))
+            for q in range(2):
+                z_rows[g, q] = rows[:, :, GROUP * q : GROUP * (q + 1)]
 
         def load_m(h):
             m_codes[h] = kept("m%d" % h, [P, 2, 2 * HALF], U8)
@@ -196,19 +203,18 @@ def tile_iv4rechubermomentmatrix_x2_kernel(tc, x, m_words, m_scales, b, y, c, z,
             t_planes[g, h] = kept("t_plane%d%d" % (g, h), [P, HALF], U8)
             quantize(t_codes[g, h][:], t_planes[g, h][:], t_woven[g, h][:])
 
-        def weave_z(g, q, engine, c0=0, c1=P):
-            if c0 == 0:
-                z_woven[g, q] = stage.tile([P, PACK * HALF], BF16, name="z_woven", bufs=3, align_bytes=64)
+        def weave_z(g, q, s, engine):
+            z_woven[g, q, s] = stage.tile([P, 2 * GROUP], BF16, name="z_woven", bufs=6, align_bytes=64)
             copy_on(
                 engine,
-                z_woven[g, q][:].rearrange("p (t m i j) -> p m t i j", t=PACK, i=2, j=PACK)[:, c0 // 2 : c1 // 2],
-                z_rows[g, q][:].rearrange("p j (m i t) -> p m t i j", i=2, t=PACK)[:, c0 // 2 : c1 // 2],
+                z_woven[g, q, s][:].rearrange("p (t m i j) -> p m t i j", t=2, i=2, j=PACK),
+                z_rows[g, q].rearrange("p j (m i t) -> p m t i j", i=2, t=PACK)[:, :, 2 * s : 2 * s + 2],
             )
 
-        def quant_z(g, q):
-            z_codes[g, q] = kept("z_codes%d%d" % (g, q), [P, GROUP], U32)
-            z_planes[g, q] = kept("z_plane%d%d" % (g, q), [P, GROUP], U8)
-            quantize(z_codes[g, q][:], z_planes[g, q][:], z_woven[g, q][:])
+        def quant_z(g, q, s):
+            z_codes[g, q, s] = kept("z_codes%d%d%d" % (g, q, s), [P, 2 * P], U32)
+            z_planes[g, q, s] = kept("z_plane%d%d%d" % (g, q, s), [P, 2 * P], U8)
+            quantize(z_codes[g, q, s][:], z_planes[g, q, s][:], z_woven[g, q, s][:])
 
         def moment(h, q, t, engine=S):
             tag, depth = (("turn_bank", 2), ("offset_bank", 3), ("residual_bank", 3) if h else ("turn_bank", 2), ("offset_bank", 3))[t]
@@ -216,8 +222,8 @@ def tile_iv4rechubermomentmatrix_x2_kernel(tc, x, m_words, m_scales, b, y, c, z,
             for g in range(2):
                 nc.tensor.matmul_mx(
                     out=bank[:],
-                    lhsT=z_codes[g, q][:, P * t : P * (t + 1)].bitcast(FP8X4),
-                    lhsT_scale=z_planes[g, q][:, P * t : P * (t + 1)],
+                    lhsT=z_codes[g, q, t // 2][:, P * (t % 2) : P * (t % 2 + 1)].bitcast(FP8X4),
+                    lhsT_scale=z_planes[g, q, t // 2][:, P * (t % 2) : P * (t % 2 + 1)],
                     rhs=t_codes[g, h][:].bitcast(FP8X4),
                     rhs_scale=t_planes[g, h][:],
                     start=(g == 0),
@@ -254,19 +260,17 @@ def tile_iv4rechubermomentmatrix_x2_kernel(tc, x, m_words, m_scales, b, y, c, z,
 
         def store_scales():
             for quad in range(4):
-                nc.scalar.dma_start(
+                nc.sync.dma_start(
                     out=out_2[:, 4 * quad : 4 * quad + 4, :].bitcast(I32),
                     in_=out_plane[32 * quad : 32 * quad + 8, :].bitcast(I32),
                 )
 
-        load_c_col(G)
-        load_m_scales(G)
         load_rows()
-        load_y(0, 0, 1)
-        load_x(0, 0, 1)
-        load_y(0, 1, 2)
-        load_x(0, 1, 2)
+        load_c_col(nc.sync)
+        load_x(0, 0, 2)
+        load_y(0, 0, 2)
         load_m(0)
+        load_m_scales(nc.sync)
         load_x(0, 2, 4)
         load_y(0, 2, 4)
         load_m(1)
@@ -274,69 +278,117 @@ def tile_iv4rechubermomentmatrix_x2_kernel(tc, x, m_words, m_scales, b, y, c, z,
         load_x(1, 0, 2)
         load_x(1, 2, 4)
         load_y(1, 0, 2)
-        load_y(1, 2, 4)
         load_z(1, 0)
+        load_y(1, 2, 4)
         load_z(0, 1)
         load_z(1, 1)
         weights()
-        for g in range(2):
-            for j in range(4):
-                if j >= min([4,2,2,2][2 * g], [4,2,2,2][2 * g + 1]):
-                    diag(g, j)
+        for j in (1, 3):
+            diag(0, j)
+        for j in range(4):
+            diag(1, j)
 
-        def x_group(g):
-            for j in range(4):
-                turn_x(g, j)
-                quant_x(g, j)
+        def pair_of_residuals(g, h, j):
+            residual(g, h, j)
+            residual(g, h, j + 1)
+            clip(g, h, j, V)
+            clip(g, h, j + 1, V)
 
-        def block(g, h, first_on_scalar):
-            for j in range(4):
-                make_offset(g, h, j, V if j < first_on_scalar else S)
-                residual(g, h, j)
-                clip(g, h, j, V)
-
-        def finish_t(g, h, first, second):
-            weave_t(g, h, first, 0, 256)
-            weave_t(g, h, second, 256, 512)
-            quant_t(g, h)
-
-        def finish_z(g, q, first, second):
-            weave_z(g, q, first, 0, 64)
-            weave_z(g, q, second, 64, 128)
-            quant_z(g, q)
-
-        def products(h, q):
-            for t in range(4):
-                moment(h, q, t)
-                if t % 2 == 1:
-                    store_out(h, q, t - 1, t + 1)
-
-        def planes(h, q):
-            weave_out(h, q, V)
-            quant_out(h, q)
-            store_words(h, q)
-
-        x_group(0)
-        block(0, 0, 4)
-        x_group(1)
-        block(0, 1, 2)
-        block(1, 0, 2)
-        finish_t(0, 0, S, V)
-        finish_z(0, 0, S, S)
-        finish_z(1, 0, S, S)
-        finish_t(1, 0, V, S)
-        products(0, 0)
-        block(1, 1, 2)
-        finish_z(0, 1, S, S)
-        finish_z(1, 1, S, S)
-        finish_t(0, 1, S, V)
-        finish_t(1, 1, V, S)
-        products(0, 1)
-        planes(0, 0)
-        products(1, 0)
-        planes(0, 1)
-        products(1, 1)
-        planes(1, 0)
+        for j in (0, 2):
+            make_offset(0, 0, j, V)
+            make_offset(0, 0, j + 1, V)
+            turn_x(0, j)
+            turn_x(0, j + 1)
+            quant_x(0, j)
+            quant_x(0, j + 1)
+            make_offset(0, 1, j, V)
+            make_offset(0, 1, j + 1, S)
+            pair_of_residuals(0, 0, j)
+        weave_z(0, 0, 0, S)
+        pair_of_residuals(0, 1, 0)
+        turn_x(1, 0)
+        turn_x(1, 1)
+        weave_z(0, 0, 1, S)
+        pair_of_residuals(0, 1, 2)
+        turn_x(1, 2)
+        turn_x(1, 3)
+        weave_t(0, 0, S)
+        quant_x(1, 0)
+        make_offset(1, 0, 0, V)
+        quant_x(1, 1)
+        make_offset(1, 0, 1, V)
+        quant_z(0, 0, 0)
+        quant_z(0, 0, 1)
+        residual(1, 0, 0)
+        quant_x(1, 2)
+        residual(1, 0, 1)
+        quant_x(1, 3)
+        make_offset(1, 0, 2, S)
+        clip(1, 0, 0, V)
+        make_offset(1, 0, 3, S)
+        clip(1, 0, 1, V)
+        weave_z(1, 0, 0, S)
+        weave_z(1, 0, 1, S)
+        pair_of_residuals(1, 0, 2)
+        make_offset(1, 1, 0, S)
+        make_offset(1, 1, 1, S)
+        weave_z(0, 1, 0, S)
+        quant_t(0, 0)
+        make_offset(1, 1, 2, S)
+        weave_t(1, 0, V)
+        make_offset(1, 1, 3, S)
+        quant_z(1, 0, 0)
+        quant_t(1, 0)
+        weave_z(1, 1, 0, S)
+        residual(1, 1, 0)
+        quant_z(1, 0, 1)
+        residual(1, 1, 1)
+        moment(0, 0, 0)
+        moment(0, 0, 1)
+        store_out(0, 0, 0, 2)
+        quant_z(0, 1, 0)
+        clip(1, 1, 0, V)
+        quant_z(1, 1, 0)
+        clip(1, 1, 1, V)
+        residual(1, 1, 2)
+        residual(1, 1, 3)
+        moment(0, 0, 2)
+        moment(0, 0, 3)
+        store_out(0, 0, 2, 4)
+        weave_t(0, 1, S)
+        weave_z(0, 1, 1, V)
+        clip(1, 1, 2, V)
+        weave_z(1, 1, 1, V)
+        clip(1, 1, 3, V)
+        moment(0, 1, 0)
+        moment(0, 1, 1)
+        store_out(0, 1, 0, 2)
+        quant_z(0, 1, 1)
+        quant_z(1, 1, 1)
+        weave_t(1, 1, V)
+        moment(0, 1, 2)
+        moment(0, 1, 3)
+        store_out(0, 1, 2, 4)
+        quant_t(0, 1)
+        quant_t(1, 1)
+        weave_out(0, 0, V, 0, 256)
+        weave_out(0, 0, V, 256, 512)
+        for t in range(4):
+            moment(1, 0, t)
+            if t % 2 == 1:
+                store_out(1, 0, t - 1, t + 1)
+        weave_out(0, 1, V)
+        quant_out(0, 0)
+        store_words(0, 0)
+        quant_out(0, 1)
+        store_words(0, 1)
+        for t in range(4):
+            moment(1, 1, t)
+            if t % 2 == 1:
+                store_out(1, 1, t - 1, t + 1)
+        weave_out(1, 0, V)
+        quant_out(1, 0)
+        store_words(1, 0)
         weave_out(1, 1, V, 0, 320)
         weave_out(1, 1, S, 320, 512)
         quant_out(1, 1)

@@ -60,10 +60,10 @@ def tile_iv4rechubermomentmatrix_x2_kernel(tc, x, m_words, m_scales, b, y, c, z,
         z_woven, z_codes, z_planes = {}, {}, {}
         results, out_woven, out_codes = {}, {}, {}
 
-        V.memset(c_row[:].bitcast(I32), 0)
-        V.memset(b_row[:].bitcast(I32), 0)
-        V.memset(m_plane[:].rearrange("p g e -> p (g e)").bitcast(I32), 0)
         make_identity(nc, ident[:])
+        V.memset(c_row[:].bitcast(I32), 0)
+        G.memset(b_row[:].bitcast(I32), 0)
+        V.memset(m_plane[:].rearrange("p g e -> p (g e)").bitcast(I32), 0)
 
         def sample_rows(src, g):
             return src[GROUP * g : GROUP * (g + 1), :].rearrange("(p j) w -> p j w", j=PACK)
@@ -207,8 +207,8 @@ def tile_iv4rechubermomentmatrix_x2_kernel(tc, x, m_words, m_scales, b, y, c, z,
             z_woven[g, q, s] = stage.tile([P, 2 * GROUP], BF16, name="z_woven", bufs=6, align_bytes=64)
             copy_on(
                 engine,
-                z_woven[g, q, s][:].rearrange("p (t m i j) -> p m t i j", t=2, i=2, j=PACK),
-                z_rows[g, q].rearrange("p j (m i t) -> p m t i j", i=2, t=PACK)[:, :, 2 * s : 2 * s + 2],
+                z_woven[g, q, s][:].rearrange("p (t m i j) -> p m j i t", t=2, i=2, j=PACK),
+                z_rows[g, q].rearrange("p j (m i t) -> p m j i t", i=2, t=PACK)[:, :, :, :, 2 * s : 2 * s + 2],
             )
 
         def quant_z(g, q, s):
@@ -265,14 +265,14 @@ def tile_iv4rechubermomentmatrix_x2_kernel(tc, x, m_words, m_scales, b, y, c, z,
                     in_=out_plane[32 * quad : 32 * quad + 8, :].bitcast(I32),
                 )
 
+        load_y(0, 0, 2)
         load_rows()
         load_c_col(nc.sync)
         load_x(0, 0, 2)
-        load_y(0, 0, 2)
+        load_y(0, 2, 4)
+        load_x(0, 2, 4)
         load_m(0)
         load_m_scales(nc.sync)
-        load_x(0, 2, 4)
-        load_y(0, 2, 4)
         load_m(1)
         load_z(0, 0)
         load_x(1, 0, 2)
@@ -297,13 +297,14 @@ def tile_iv4rechubermomentmatrix_x2_kernel(tc, x, m_words, m_scales, b, y, c, z,
         for j in (0, 2):
             make_offset(0, 0, j, V)
             make_offset(0, 0, j + 1, V)
+            make_offset(0, 1, j, V)
             turn_x(0, j)
             turn_x(0, j + 1)
+            make_offset(0, 1, j + 1, S)
             quant_x(0, j)
             quant_x(0, j + 1)
-            make_offset(0, 1, j, V)
-            make_offset(0, 1, j + 1, S)
-            pair_of_residuals(0, 0, j)
+        pair_of_residuals(0, 0, 0)
+        pair_of_residuals(0, 0, 2)
         weave_z(0, 0, 0, S)
         pair_of_residuals(0, 1, 0)
         turn_x(1, 0)
@@ -339,23 +340,22 @@ def tile_iv4rechubermomentmatrix_x2_kernel(tc, x, m_words, m_scales, b, y, c, z,
         make_offset(1, 1, 3, S)
         quant_z(1, 0, 0)
         quant_t(1, 0)
-        weave_z(1, 1, 0, S)
         residual(1, 1, 0)
         quant_z(1, 0, 1)
         residual(1, 1, 1)
         moment(0, 0, 0)
         moment(0, 0, 1)
         store_out(0, 0, 0, 2)
+        weave_z(1, 1, 0, S)
         quant_z(0, 1, 0)
         clip(1, 1, 0, V)
-        quant_z(1, 1, 0)
         clip(1, 1, 1, V)
         residual(1, 1, 2)
         residual(1, 1, 3)
+        quant_z(1, 1, 0)
         moment(0, 0, 2)
         moment(0, 0, 3)
         store_out(0, 0, 2, 4)
-        weave_t(0, 1, S)
         weave_z(0, 1, 1, V)
         clip(1, 1, 2, V)
         weave_z(1, 1, 1, V)
@@ -363,34 +363,33 @@ def tile_iv4rechubermomentmatrix_x2_kernel(tc, x, m_words, m_scales, b, y, c, z,
         moment(0, 1, 0)
         moment(0, 1, 1)
         store_out(0, 1, 0, 2)
+        weave_t(0, 1, S)
         quant_z(0, 1, 1)
         quant_z(1, 1, 1)
         weave_t(1, 1, V)
         moment(0, 1, 2)
         moment(0, 1, 3)
         store_out(0, 1, 2, 4)
-        quant_t(0, 1)
         quant_t(1, 1)
-        weave_out(0, 0, V, 0, 256)
-        weave_out(0, 0, V, 256, 512)
+        quant_t(0, 1)
+        weave_out(0, 0, V)
         for t in range(4):
             moment(1, 0, t)
-            if t % 2 == 1:
-                store_out(1, 0, t - 1, t + 1)
+            store_out(1, 0, t, t + 1)
         weave_out(0, 1, V)
         quant_out(0, 0)
         store_words(0, 0)
-        quant_out(0, 1)
-        store_words(0, 1)
         for t in range(4):
             moment(1, 1, t)
             if t % 2 == 1:
                 store_out(1, 1, t - 1, t + 1)
         weave_out(1, 0, V)
+        quant_out(0, 1)
+        store_words(0, 1)
         quant_out(1, 0)
         store_words(1, 0)
-        weave_out(1, 1, V, 0, 320)
-        weave_out(1, 1, S, 320, 512)
+        weave_out(1, 1, V, 0, 256)
+        weave_out(1, 1, S, 256, 512)
         quant_out(1, 1)
         store_words(1, 1)
         store_scales()

from contextlib import ExitStack

import concourse.mybir as mybir
from concourse.masks import make_identity

B, D, E, Q = 1024, 1024, 1024, 1024
FLOPS = 2 * B * D * E + 2 * B * Q * E

F32 = mybir.dt.float32
BF16 = mybir.dt.bfloat16
I32 = mybir.dt.int32
U32 = mybir.dt.uint32
U8 = mybir.dt.uint8
FP8X4 = mybir.dt.float8_e4m3fn_x4
FP4X4 = mybir.dt.float4_e2m1fn_x4
ALU = mybir.AluOpType
ACT = mybir.ActivationFunctionType

P = 128
PACK = 4
GROUP = P * PACK
HALF = 512
OUT_SCALE = 1.0 / 32.0


def tile_iv4rechubermomentmatrix_x2_kernel(tc, x, m_words, m_scales, b, y, c, z, out_0, out_1, out_2):
    nc = tc.nc
    V, S, G = nc.vector, nc.scalar, nc.gpsimd

    with ExitStack() as ctx:
        keep = ctx.enter_context(tc.tile_pool(name="keep", bufs=1))
        stage = ctx.enter_context(tc.tile_pool(name="stage", bufs=3))
        psum = ctx.enter_context(tc.psum_pool(name="psum", bufs=1))
        ctx.enter_context(tc.manual_schedule())

        def kept(name, shape, dtype):
            return keep.tile(shape, dtype, name=name, align_bytes=64)

        def copy_on(engine, out, in_):
            if engine is S:
                S.copy(out=out, in_=in_)
            elif engine is G:
                G.tensor_scalar(out=out, in0=in_, scalar1=1.0, scalar2=0.0, op0=ALU.mult, op1=ALU.add)
            else:
                V.tensor_copy(out=out, in_=in_)

        ident = kept("ident", [P, P], F32)
        c_row = kept("c_row", [P, B], BF16)
        b_row = kept("b_row", [P, E], BF16)
        c_col = kept("c_col", [P, 2 * PACK], BF16)
        c_neg = kept("c_neg", [P, 2 * PACK], F32)
        c_abs = kept("c_abs", [P, 2 * PACK], F32)
        c_abs_neg = kept("c_abs_neg", [P, 2 * PACK], F32)
        m_plane = kept("m_plane", [P, 2, E], U8)
        out_plane = kept("out_plane", [P, E], U8)

        x_rows, y_rows, z_rows, m_codes, diags = {}, {}, {}, {}, {}
        x_woven, x_codes, x_planes = {}, {}, {}
        offsets, scaled, t_rows, t_woven, t_codes, t_planes = {}, {}, {}, {}, {}, {}
        z_woven, z_codes, z_planes = {}, {}, {}
        results, out_woven, out_codes = {}, {}, {}

        make_identity(nc, ident[:])
        V.memset(c_row[:].bitcast(I32), 0)
        G.memset(b_row[:].bitcast(I32), 0)
        V.memset(m_plane[:].rearrange("p g e -> p (g e)").bitcast(I32), 0)

        def sample_rows(src, g):
            return src[GROUP * g : GROUP * (g + 1), :].rearrange("(p j) w -> p j w", j=PACK)

        def load_rows():
            nc.sync.dma_start(out=c_row[0:1, :], in_=c.rearrange("(o n) -> o n", o=1))
            nc.sync.dma_start(out=b_row[0:1, :], in_=b.rearrange("(o n) -> o n", o=1))

        def load_c_col(engine):
            engine.dma_start(
                out=c_col[:].rearrange("p (g j) -> p g j", g=2),
                in_=c.rearrange("(g p j) -> p g j", g=2, j=PACK),
            )

        def load_slots(src, name, table, g, j0, j1):
            rows = kept("%s%d%d" % (name, g, j0), [P, j1 - j0, src.shape[1]], BF16)
            nc.sync.dma_start(out=rows[:], in_=sample_rows(src, g)[:, j0:j1, :])
            for j in range(j0, j1):
                table[g, j] = rows[:, j - j0, :]

        def load_x(g, j0, j1):
            load_slots(x, "x", x_rows, g, j0, j1)

        def load_y(g, j0, j1):
            load_slots(y, "y", y_rows, g, j0, j1)

        def load_z(g, q):
            rows = kept("z%d%d" % (g, q), [P, PACK, GROUP], BF16)
            z_rows[g, q] = rows[:]
            nc.sync.dma_start(out=rows[:], in_=sample_rows(z, g)[:, :, GROUP * q : GROUP * (q + 1)])

        def load_z_group(g):
            rows = kept("z%d" % g, [P, PACK, Q], BF16)
            nc.sync.dma_start(out=rows[:], in_=sample_rows(z, g))
            for q in range(2):
                z_rows[g, q] = rows[:, :, GROUP * q : GROUP * (q + 1)]

        def load_m(h):
            m_codes[h] = kept("m%d" % h, [P, 2, 2 * HALF], U8)
            src = m_words.rearrange("k p w -> p k w")[:, :, 2 * HALF * h : 2 * HALF * (h + 1)]
            nc.sync.dma_start(out=m_codes[h][:].bitcast(I32), in_=src.bitcast(I32))

        def load_m_scales(engine):
            for quad in range(4):
                src = m_scales[:, 4 * quad : 4 * quad + 4, :].rearrange("k r e -> r k e")
                engine.dma_start(out=m_plane[32 * quad : 32 * quad + 4, :, :].bitcast(I32), in_=src.bitcast(I32))

        def weights():
            S.activation(out=c_abs[:], in_=c_col[:], func=ACT.Abs)
            V.tensor_scalar(out=c_neg[:], in0=c_col[:], scalar1=-1.0, scalar2=None, op0=ALU.mult)
            V.tensor_scalar(out=c_abs_neg[:], in0=c_abs[:], scalar1=-1.0, scalar2=None, op0=ALU.mult)

        def column(tile, g, j):
            return tile[:, PACK * g + j : PACK * g + j + 1]

        def diag(g, j):
            diags[g, j] = kept("diag%d%d" % (g, j), [P, P], BF16)
            V.tensor_scalar(out=diags[g, j][:], in0=ident[:], scalar1=column(c_neg, g, j), scalar2=None, op0=ALU.mult)

        def make_offset(g, h, j, engine):
            cols = slice(HALF * h, HALF * (h + 1))
            bank = psum.tile([P, HALF], F32, name="offset_bank", bufs=3)
            offsets[g, h, j] = kept("offset%d%d%d" % (g, h, j), [P, HALF], F32)
            c_slot = c_row[:, GROUP * g + j : GROUP * (g + 1) : PACK]
            if engine is S:
                nc.tensor.matmul(bank[:], lhsT=c_slot, rhs=b_row[:, cols], start=True, stop=False)
                nc.tensor.matmul(bank[:], lhsT=diags[g, j][:], rhs=y_rows[g, j][:, cols], start=False, stop=True)
                S.copy(out=offsets[g, h, j][:], in_=bank[:])
            else:
                nc.tensor.matmul(bank[:], lhsT=c_slot, rhs=b_row[:, cols], start=True, stop=True)
                V.scalar_tensor_tensor(
                    out=offsets[g, h, j][:], in0=y_rows[g, j][:, cols], scalar=column(c_neg, g, j),
                    in1=bank[:], op0=ALU.mult, op1=ALU.add,
                )

        def turn_x(g, j):
            bank = psum.tile([P, HALF], F32, name="turn_bank", bufs=2)
            pairs = x_rows[g, j].bitcast(F32)
            for k in range(2):
                for u in range(2):
                    at = P * (2 * k + u)
                    nc.tensor.transpose(bank[:, at : at + P], pairs[:, 256 * k + u : 256 * (k + 1) : 2], ident[:])
            x_woven[g, j] = stage.tile([P, D], BF16, name="x_woven", bufs=4, align_bytes=64)
            S.copy(
                out=x_woven[g, j][:].bitcast(F32).rearrange("p (k n u) -> p k n u", k=2, u=2),
                in_=bank[:].rearrange("p (k u n) -> p k n u", k=2, u=2),
            )

        def quantize(codes, plane, woven):
            V.quantize_mx(out=codes.bitcast(FP8X4), scales=plane, in_=woven)

        def quant_x(g, j):
            x_codes[g, j] = kept("x_codes%d%d" % (g, j), [P, 2 * P], U32)
            x_planes[g, j] = kept("x_plane%d%d" % (g, j), [P, 2 * P], U8)
            quantize(x_codes[g, j][:], x_planes[g, j][:], x_woven[g, j][:])

        def residual(g, h, j):
            bank = psum.tile([P, HALF], F32, name="residual_bank", bufs=3)
            for k in range(2):
                nc.tensor.matmul_mx(
                    out=bank[:],
                    lhsT=x_codes[g, j][:, P * k : P * (k + 1)].bitcast(FP8X4),
                    lhsT_scale=x_planes[g, j][:, P * k : P * (k + 1)],
                    rhs=m_codes[h][:, k, :].bitcast(FP4X4),
                    rhs_scale=m_plane[:, k, HALF * h : HALF * (h + 1)],
                    start=(k == 0),
                    stop=(k == 1),
                )
            scaled[g, h, j] = stage.tile([P, HALF], F32, name="scaled", bufs=4)
            V.scalar_tensor_tensor(
                out=scaled[g, h, j][:], in0=bank[:], scalar=column(c_col, g, j),
                in1=offsets[g, h, j][:], op0=ALU.mult, op1=ALU.add,
            )

        def clip(g, h, j, engine=V):
            if j == 0:
                t_rows[g, h] = stage.tile([P, PACK, HALF], BF16, name="t_rows", bufs=3)
            engine.tensor_scalar(
                out=t_rows[g, h][:, j, :], in0=scaled[g, h, j][:],
                scalar1=column(c_abs, g, j), scalar2=column(c_abs_neg, g, j), op0=ALU.min, op1=ALU.max,
            )

        def weave(engine, woven, rows, c0, c1):
            copy_on(
                engine,
                woven[:].rearrange("p (w i j) -> p w j i", i=4, j=PACK)[:, c0 // 4 : c1 // 4],
                rows[:].rearrange("p j (w i) -> p w j i", i=4)[:, c0 // 4 : c1 // 4],
            )

        def weave_t(g, h, engine, c0=0, c1=HALF):
            if c0 == 0:
                t_woven[g, h] = stage.tile([P, PACK * HALF], BF16, name="t_woven", bufs=2, align_bytes=64)
            weave(engine, t_woven[g, h], t_rows[g, h], c0, c1)

        def quant_t(g, h):
            t_codes[g, h] = kept("t_codes%d%d" % (g, h), [P, HALF], U32)
            t_planes[g, h] = kept("t_plane%d%d" % (g, h), [P, HALF], U8)
            quantize(t_codes[g, h][:], t_planes[g, h][:], t_woven[g, h][:])

        def weave_z(g, q, s, engine):
            z_woven[g, q, s] = stage.tile([P, 2 * GROUP], BF16, name="z_woven", bufs=6, align_bytes=64)
            copy_on(
                engine,
                z_woven[g, q, s][:].rearrange("p (t m i j) -> p m j i t", t=2, i=2, j=PACK),
                z_rows[g, q].rearrange("p j (m i t) -> p m j i t", i=2, t=PACK)[:, :, :, :, 2 * s : 2 * s + 2],
            )

        def quant_z(g, q, s):
            z_codes[g, q, s] = kept("z_codes%d%d%d" % (g, q, s), [P, 2 * P], U32)
            z_planes[g, q, s] = kept("z_plane%d%d%d" % (g, q, s), [P, 2 * P], U8)
            quantize(z_codes[g, q, s][:], z_planes[g, q, s][:], z_woven[g, q, s][:])

        def moment(h, q, t, engine=S):
            tag, depth = (("turn_bank", 2), ("offset_bank", 3), ("residual_bank", 3) if h else ("turn_bank", 2), ("offset_bank", 3))[t]
            bank = psum.tile([P, HALF], F32, name=tag, bufs=depth)
            for g in range(2):
                nc.tensor.matmul_mx(
                    out=bank[:],
                    lhsT=z_codes[g, q, t // 2][:, P * (t % 2) : P * (t % 2 + 1)].bitcast(FP8X4),
                    lhsT_scale=z_planes[g, q, t // 2][:, P * (t % 2) : P * (t % 2 + 1)],
                    rhs=t_codes[g, h][:].bitcast(FP8X4),
                    rhs_scale=t_planes[g, h][:],
                    start=(g == 0),
                    stop=(g == 1),
                )
            if t == 0:
                results[h, q] = kept("result%d%d" % (h, q), [P, PACK, HALF], F32)
            if engine is S:
                S.activation(out=results[h, q][:, t, :], in_=bank[:], func=ACT.Copy, scale=OUT_SCALE)
            else:
                V.tensor_scalar(out=results[h, q][:, t, :], in0=bank[:], scalar1=OUT_SCALE, scalar2=None, op0=ALU.mult)

        def store_out(h, q, t0, t1):
            dst = sample_rows(out_0, q)[:, t0:t1, HALF * h : HALF * (h + 1)]
            nc.sync.dma_start(out=dst, in_=results[h, q][:, t0:t1, :])

        def weave_out(h, q, engine, c0=0, c1=HALF):
            if c0 == 0:
                out_woven[h, q] = stage.tile([P, PACK * HALF], BF16, name="out_woven", bufs=3, align_bytes=64)
            weave(engine, out_woven[h, q], results[h, q], c0, c1)

        def quant_out(h, q, c0=0, c1=HALF):
            if c0 == 0:
                out_codes[h, q] = kept("out_codes%d%d" % (h, q), [P, HALF], U32)
            quantize(
                out_codes[h, q][:, c0:c1],
                out_plane[4 * q : P, HALF * h + c0 : HALF * h + c1],
                out_woven[h, q][:, PACK * c0 : PACK * c1],
            )

        def store_words(h, q, c0=0, c1=HALF):
            dst = out_1[q].rearrange("p e t -> p (e t)")[:, PACK * (HALF * h + c0) : PACK * (HALF * h + c1)]
            nc.sync.dma_start(out=dst.bitcast(I32), in_=out_codes[h, q][:, c0:c1].bitcast(I32))

        def store_scales():
            for quad in range(4):
                nc.sync.dma_start(
                    out=out_2[:, 4 * quad : 4 * quad + 4, :].bitcast(I32),
                    in_=out_plane[32 * quad : 32 * quad + 8, :].bitcast(I32),
                )

        load_y(0, 0, 2)
        load_rows()
        load_c_col(nc.sync)
        load_x(0, 0, 2)
        load_y(0, 2, 4)
        load_x(0, 2, 4)
        load_m(0)
        load_m_scales(nc.sync)
        load_m(1)
        load_z(0, 0)
        load_x(1, 0, 2)
        load_x(1, 2, 4)
        load_y(1, 0, 2)
        load_z(1, 0)
        load_y(1, 2, 4)
        load_z(0, 1)
        load_z(1, 1)
        weights()
        for j in (1, 3):
            diag(0, j)
        for j in range(4):
            diag(1, j)

        def pair_of_residuals(g, h, j):
            residual(g, h, j)
            residual(g, h, j + 1)
            clip(g, h, j, V)
            clip(g, h, j + 1, V)

        for j in (0, 2):
            make_offset(0, 0, j, V)
            make_offset(0, 0, j + 1, V)
            make_offset(0, 1, j, V)
            turn_x(0, j)
            turn_x(0, j + 1)
            make_offset(0, 1, j + 1, S)
            quant_x(0, j)
            quant_x(0, j + 1)
        pair_of_residuals(0, 0, 0)
        pair_of_residuals(0, 0, 2)
        weave_z(0, 0, 0, S)
        pair_of_residuals(0, 1, 0)
        turn_x(1, 0)
        turn_x(1, 1)
        weave_z(0, 0, 1, S)
        pair_of_residuals(0, 1, 2)
        turn_x(1, 2)
        turn_x(1, 3)
        weave_t(0, 0, S)
        quant_x(1, 0)
        make_offset(1, 0, 0, V)
        quant_x(1, 1)
        make_offset(1, 0, 1, V)
        quant_z(0, 0, 0)
        quant_z(0, 0, 1)
        residual(1, 0, 0)
        quant_x(1, 2)
        residual(1, 0, 1)
        quant_x(1, 3)
        make_offset(1, 0, 2, S)
        clip(1, 0, 0, V)
        make_offset(1, 0, 3, S)
        clip(1, 0, 1, V)
        weave_z(1, 0, 0, S)
        weave_z(1, 0, 1, S)
        pair_of_residuals(1, 0, 2)
        make_offset(1, 1, 0, S)
        make_offset(1, 1, 1, S)
        weave_z(0, 1, 0, S)
        quant_t(0, 0)
        make_offset(1, 1, 2, S)
        weave_t(1, 0, V)
        make_offset(1, 1, 3, S)
        quant_z(1, 0, 0)
        quant_t(1, 0)
        residual(1, 1, 0)
        quant_z(1, 0, 1)
        residual(1, 1, 1)
        moment(0, 0, 0)
        moment(0, 0, 1)
        store_out(0, 0, 0, 2)
        weave_z(1, 1, 0, S)
        quant_z(0, 1, 0)
        clip(1, 1, 0, V)
        clip(1, 1, 1, V)
        residual(1, 1, 2)
        residual(1, 1, 3)
        quant_z(1, 1, 0)
        moment(0, 0, 2)
        moment(0, 0, 3)
        store_out(0, 0, 2, 4)
        weave_z(0, 1, 1, V)
        clip(1, 1, 2, V)
        weave_z(1, 1, 1, V)
        clip(1, 1, 3, V)
        moment(0, 1, 0)
        moment(0, 1, 1)
        store_out(0, 1, 0, 2)
        weave_t(0, 1, S)
        quant_z(0, 1, 1)
        quant_z(1, 1, 1)
        weave_t(1, 1, V)
        moment(0, 1, 2)
        moment(0, 1, 3)
        store_out(0, 1, 2, 4)
        quant_t(1, 1)
        quant_t(0, 1)
        weave_out(0, 0, V)
        for t in range(4):
            moment(1, 0, t)
            store_out(1, 0, t, t + 1)
        weave_out(0, 1, V)
        quant_out(0, 0)
        store_words(0, 0)
        for t in range(4):
            moment(1, 1, t)
            if t % 2 == 1:
                store_out(1, 1, t - 1, t + 1)
        weave_out(1, 0, V)
        quant_out(0, 1)
        store_words(0, 1)
        quant_out(1, 0)
        store_words(1, 0)
        weave_out(1, 1, V, 0, 256)
        weave_out(1, 1, S, 256, 512)
        quant_out(1, 1)
        store_words(1, 1)
        store_scales()
